import numpy as np
import ml_dtypes


def mxq(x, axis, fmt="e4m3"):
    dtype, down = {"e4m3": (ml_dtypes.float8_e4m3fn, 7), "e5m2": (ml_dtypes.float8_e5m2, 14)}[fmt]
    v = np.moveaxis(np.asarray(x, np.float32).astype(ml_dtypes.bfloat16).astype(np.float64), axis, -1)
    blocks = v.reshape(v.shape[:-1] + (-1, 32))
    amax = np.abs(blocks).max(-1, keepdims=True)
    byte = np.maximum(np.where(amax > 0, np.frexp(amax)[1] - 1 + 127, 0) - down, 1)
    scale = np.exp2(byte - 127.0)
    codes = (blocks / scale).astype(np.float32).astype(dtype).astype(np.float64)
    return np.moveaxis((codes * scale).reshape(v.shape), -1, axis)


WIDE = False


def mx_kscale(k):
    if not WIDE:
        return np.ones(k)
    levels = np.array([10, -10, 5, -5, 0])
    if k % 512:
        return np.exp2(np.random.permutation(np.resize(levels, k // 32))).repeat(32)
    a = np.empty((k // 512, 16))
    for p in range(k // 512):
        a[p, :8] = np.random.permutation(np.resize(levels, 8))
        for g in range(8):
            far = levels[np.abs(levels - a[p, g]) >= 10]
            a[p, g + 8] = far[np.random.randint(len(far))]
    return np.exp2(a.ravel()).repeat(32)


def f64(x):
    return np.asarray(x).astype(np.float64)


def striped(idx):
    return np.tile(np.asarray(idx).reshape(-1, 16).T, (8, 1)).astype(np.uint16)


def unstriped(offs):
    return offs[:16].T.reshape(-1).astype(np.int64)


E2M1 = np.array([0.0, 0.5, 1.0, 1.5, 2.0, 3.0, 4.0, 6.0, -0.0, -0.5, -1.0, -1.5, -2.0, -3.0, -4.0, -6.0])


def pack_weight(w, fmt):
    k, n = w.shape
    w = f64(np.asarray(w, np.float32).astype(ml_dtypes.bfloat16)).reshape(k // 32, 32, n)
    amax = np.abs(w).max(1)
    if fmt == "e4m3":
        byte = np.frexp(amax)[1] - 1 + 127 - 7
    else:
        mant, ex = np.frexp(amax / 6.0)
        byte = np.where(mant > 0.5, ex, ex - 1) + 127
    byte = np.clip(np.where(amax > 0, byte, 1), 1, 254)
    scaled = (w * np.exp2(127.0 - byte)[:, None, :]).reshape(k, n).astype(np.float32)
    by_word = np.ascontiguousarray(scaled.reshape(k // 512, 128, 4, n).transpose(0, 1, 3, 2))
    if fmt == "e4m3":
        words = by_word.astype(ml_dtypes.float8_e4m3fn).view(np.uint8)
    else:
        c = by_word.astype(ml_dtypes.float4_e2m1fn).view(np.uint8) & 0xF
        words = (c[..., 0::2] | (c[..., 1::2] << 4)).reshape(k // 512, 128, 2 * n)
    return np.ascontiguousarray(words), np.ascontiguousarray(byte.astype(np.uint8).reshape(k // 512, 16, n))


def unpack_weight(words, scales, fmt):
    g, _, n = scales.shape
    words = np.ascontiguousarray(words).reshape(g, 128, n, -1)
    if fmt == "e4m3":
        vals = words.view(ml_dtypes.float8_e4m3fn).astype(np.float64)
    else:
        nib = np.empty((g, 128, n, 4), np.uint8)
        nib[..., 0::2] = words & 0xF
        nib[..., 1::2] = words >> 4
        vals = E2M1[nib]
    vals = vals * np.repeat(np.exp2(scales.astype(np.float64) - 127.0), 8, axis=1)[..., None]
    return vals.transpose(0, 1, 3, 2).reshape(g * 512, n)


def softplus(v):
    return np.log(1.0 + np.exp(v))


def sigmoid(v):
    return 1.0 / (1.0 + np.exp(-v))


D, E, T, I, Q, G = 512, 512, 2048, 512, 128, 64


def setup_inputs():
    n = np.random.standard_normal
    idx = np.random.permutation(T)[:I]
    fd = mx_kscale(D)
    fe = mx_kscale(E)
    keysp = pack_weight(n((D, T)) / fd[:, None], "e4m3")
    valsp = pack_weight(n((E, T)) / fe[:, None], "e4m3")
    return {
        "query": (n((D, Q)) * 0.8 / np.sqrt(D) * fd[:, None]).astype(np.float32),
        "query2": (n((D, Q)) * 1.0 / np.sqrt(D) * fd[:, None]).astype(np.float32),
        "keys_words": keysp[0],
        "keys_scales": keysp[1],
        "reserve": (np.random.uniform(2.0, 10.0, (Q, 1))).astype(np.float32),
        "gout": (n((E, Q)) * 1 / np.sqrt(E) * fe[:, None]).astype(np.float32),
        "vals_words": valsp[0],
        "vals_scales": valsp[1],
        "dquery2": (n((D, Q)) * 1.0 / np.sqrt(D) * fd[:, None]).astype(np.float32),
        "base": (0.5 * n((Q, T))).astype(np.float32),
        "offs": striped(idx),
    }


def reference(query, query2, keys_words, keys_scales, reserve, gout, vals_words, vals_scales, dquery2, base, offs):
    idx = unstriped(offs)
    keysu = unpack_weight(keys_words, keys_scales, "e4m3")
    valsu = unpack_weight(vals_words, vals_scales, "e4m3")
    queryq = mxq(f64(query), 0, "e4m3")
    keysidxg = keysu[:, idx]
    a = queryq.T @ keysidxg
    query2q = mxq(f64(query2), 0, "e4m3")
    b = query2q.T @ keysidxg
    dquery2q = mxq(f64(dquery2), 0, "e4m3")
    tb = dquery2q.T @ keysidxg
    m1 = b.reshape(Q, G, I // G).mean(axis=2)
    q0 = softplus(m1 * 3.0)
    z = np.sum(q0, axis=1, keepdims=True) + f64(reserve)
    pa = np.exp(a)
    s = pa.reshape(Q, G, I // G).sum(axis=2)
    goutq = mxq(f64(gout), 0, "e4m3")
    valsidxg = valsu[:, idx]
    c0 = goutq.T @ valsidxg
    drr = c0 * pa
    dr = drr.reshape(Q, G, I // G).sum(axis=2)
    dz = np.sum(dr * q0 / s / np.square(z) * (-1.0), axis=1, keepdims=True)
    dq0 = dr / z / s + dz
    tm1 = tb.reshape(Q, G, I // G).mean(axis=2)
    tq0 = tm1 * 3.0 * sigmoid(m1 * 3.0)
    tz = np.sum(tq0, axis=1, keepdims=True)
    tdz = np.sum((tq0 / s * dr - tz * z * 2.0 * dr * q0 / s / np.square(z)) / np.square(z) * (-1.0), axis=1, keepdims=True)
    tdq0 = tz * dr / np.square(z) * (-1.0) / s + tdz
    tdm1 = (tdq0 * sigmoid(m1 * 3.0) + tm1 * 3.0 * sigmoid(m1 * 3.0) * (1.0 - sigmoid(m1 * 3.0)) * dq0) * 3.0
    te1 = tdm1 / 8.0
    tr1 = np.repeat(te1, I // G, axis=1)
    gs = tr1 * 1024.0
    gf = np.zeros((Q, T))
    gf[:, idx] = gs
    y = f64(base) + gf
    return y

@@ -1,0 +1,222 @@
+from contextlib import ExitStack
+
+import concourse.mybir as mybir
+
+F32 = mybir.dt.float32
+BF16 = mybir.dt.bfloat16
+I32 = mybir.dt.int32
+U32 = mybir.dt.uint32
+U16 = mybir.dt.uint16
+U8 = mybir.dt.uint8
+FP8X4 = mybir.dt.float8_e4m3fn_x4
+ALU = mybir.AluOpType
+ACT = mybir.ActivationFunctionType
+AX = mybir.AxisListType
+
+P = 128
+PACK = 4
+T = 2048
+SLOTS = 512
+Q = 128
+PAGES = 64
+PAGE = 8
+RUNS = 4
+PAIR = PAGE // RUNS
+RUN = SLOTS // RUNS
+OUT_WIDTHS = (512, 512, 512, 512)
+VAL_PLANE = 4
+
+FLOPS = 4 * 2 * 512 * Q * SLOTS
+
+
+def tile_attend_hvpagequotas_s_kernel(
+    tc, query, query2, keys_words, keys_scales, reserve, gout, vals_words, vals_scales, dquery2, base, offs, out
+):
+    nc = tc.nc
+    with ExitStack() as ctx:
+        lists = ctx.enter_context(tc.tile_pool(name="lists", bufs=1))
+        sb = ctx.enter_context(tc.tile_pool(name="sb", bufs=1))
+        psum = ctx.enter_context(tc.psum_pool(name="psum", bufs=1))
+
+        def small(name, cols=PAGES, tag=None):
+            return sb.tile([P, cols], F32, name=name, tag=tag or name)
+
+        def per_slot(ap):
+            return ap.unsqueeze(2).to_broadcast([P, PAGES, PAGE])
+
+        def by_page(ap):
+            return ap.rearrange("p (g j) -> p g j", j=PAGE)
+
+        def dealt(ap):
+            return ap.rearrange("p (h g l) -> p g h l", h=RUNS, l=PAIR)
+
+        offsets = lists.tile([P, SLOTS // 16], U16, name="offsets")
+        nc.sync.dma_start(offsets[:], offs)
+
+        def load_scales(queue, name, scales, first_row):
+            plane = sb.tile([P, T], U8, name=name, align_bytes=64)
+            nc.vector.memset(plane[:].bitcast(I32), 0)
+            for quad in range(4):
+                r0 = 32 * quad + first_row
+                queue.dma_start(
+                    out=plane[r0 : r0 + 4, :].bitcast(I32), in_=scales[0, 4 * quad : 4 * quad + 4, :].bitcast(I32)
+                )
+            return plane
+
+        def load_words(name, words):
+            pool_words = sb.tile([P, T], I32, name=name, tag=name, align_bytes=64)
+            nc.sync.dma_start(out=pool_words[:], in_=words[0].rearrange("p n t -> p (n t)").bitcast(I32))
+            return pool_words
+
+        def load_rows(queue, name, rows):
+            raw = sb.tile([P, PACK, Q], F32, name=name, tag=name)
+            queue.dma_start(out=raw[:], in_=rows.rearrange("(p j) w -> p j w", j=PACK))
+            return raw
+
+        key_pool = load_words("key_pool", keys_words)
+        key_plane = load_scales(nc.scalar, "key_plane", keys_scales, 0)
+        raw_a = load_rows(nc.sync, "raw_a", query)
+        raw_b = load_rows(nc.sync, "raw_b", query2)
+        val_plane = load_scales(nc.sync, "val_plane", vals_scales, VAL_PLANE)
+        raw_tb = load_rows(nc.sync, "raw_tb", dquery2)
+        raw_c = load_rows(nc.sync, "raw_c", gout)
+        val_pool = load_words("val_pool", vals_words)
+        res = small("res", 1)
+        nc.sync.dma_start(out=res[:], in_=reserve)
+        base_sb = sb.tile([P, T], F32, name="base_sb")
+        nc.sync.dma_start(out=base_sb[:], in_=base)
+
+        placed = sb.tile([P, T], F32, name="placed")
+        nc.vector.memset(placed[:], 0.0)
+        half = small("half", 1)
+        nc.vector.memset(half[:], 0.5)
+
+        def gather(name, window, dtype, order):
+            picked = sb.tile([P, SLOTS], dtype, name=name, align_bytes=64)
+            nc.vector.tensor_copy(order(picked[:]), window.indirect(offsets[:]))
+            return picked
+
+        def as_listed(ap):
+            return ap
+
+        def quantize(name, raw):
+            grouped = sb.tile([P, Q, PACK], BF16, name=name + "_grouped", align_bytes=64)
+            nc.scalar.activation(grouped[:], raw[:].rearrange("p j w -> p w j"), ACT.Copy)
+            codes = sb.tile([P, Q], U32, name=name + "_codes", align_bytes=64)
+            scales = sb.tile([P, Q], U8, name=name + "_scales", align_bytes=64)
+            nc.vector.quantize_mx(
+                out=codes[:].bitcast(FP8X4), scales=scales[:], in_=grouped[:].rearrange("p w j -> p (w j)")
+            )
+            return codes, scales
+
+        def product(acc, rows, words, plane, start=True, stop=True):
+            nc.tensor.matmul_mx(
+                out=acc,
+                lhsT=rows[0][:].bitcast(FP8X4),
+                lhsT_scale=rows[1][:],
+                rhs=words.bitcast(FP8X4),
+                rhs_scale=plane,
+                start=start,
+                stop=stop,
+            )
+
+        key_bytes = gather("key_bytes", key_plane[:], U8, dealt)
+        key_codes = gather("key_codes", key_pool[:].bitcast(U32), U32, dealt)
+        a = psum.tile([Q, SLOTS], F32, name="a")
+        product(a[:], quantize("qa", raw_a), key_codes[:], key_bytes[:])
+        pairs = psum.tile([Q, 2, RUN], F32, name="pairs")
+        for side, (name, raw) in enumerate((("qb", raw_b), ("qt", raw_tb))):
+            rows = quantize(name, raw)
+            for h in range(RUNS):
+                cols = slice(h * RUN, (h + 1) * RUN)
+                product(pairs[:, side, :], rows, key_codes[:, cols], key_bytes[:, cols], h == 0, h == RUNS - 1)
+
+        val_bytes = gather("val_bytes", val_plane[:], U8, as_listed)
+
+        rows_c = quantize("qc", raw_c)
+        top = small("top")
+        shifted = small("shifted", SLOTS, tag="exp_arg")
+        nc.vector.tensor_reduce(top[:], dealt(a[:]), AX.XY, ALU.max)
+        nc.vector.tensor_tensor(
+            shifted[:].rearrange("p (g h l) -> p g h l", h=RUNS, l=PAIR),
+            dealt(a[:]),
+            top[:].unsqueeze(2).unsqueeze(3).to_broadcast([P, PAGES, RUNS, PAIR]),
+            ALU.subtract,
+        )
+        pa = small("pa", SLOTS)
+        nc.scalar.activation(pa[:], shifted[:], ACT.Exp)
+
+        sums = small("sums", 2 * PAGES)
+        nc.vector.tensor_reduce(sums[:], pairs[:].rearrange("p s (g l) -> p (s g) l", l=PAIR), AX.X, ALU.add)
+        sum_b = sums[:, :PAGES]
+        sum_tb = sums[:, PAGES:]
+        th = small("th")
+        nc.scalar.activation(th[:], sum_b, ACT.Tanh, scale=0.1875)
+        pos = small("pos")
+        pos_sum = small("pos_sum", 1)
+        nc.scalar.activation(pos[:], sum_b, ACT.Relu, scale=0.375, accum_out=pos_sum[:])
+        abs_th = small("abs_th", tag="raw_c")
+        nc.scalar.activation(abs_th[:], th[:], ACT.Abs)
+        sig = small("sig")
+        nc.scalar.activation(sig[:], th[:], ACT.Identity, bias=half[:], scale=0.5)
+        z_pos = small("z_pos", 1)
+        nc.scalar.activation(z_pos[:], pos_sum[:], ACT.Identity, bias=res[:], scale=1.0)
+        log_sig = small("log_sig", tag="exp_arg")
+        log_sum = small("log_sum", 1)
+        nc.scalar.activation(log_sig[:], abs_th[:], ACT.Ln, bias=half[:], scale=0.5, accum_out=log_sum[:])
+
+        s = small("s")
+        nc.vector.tensor_reduce(s[:], by_page(pa[:]), AX.X, ALU.add)
+        inv_s = small("inv_s")
+        log_s = small("log_s", tag="late")
+        nc.scalar.activation(log_s[:], s[:], ACT.Ln)
+        nc.scalar.activation(inv_s[:], log_s[:], ACT.Exp, scale=-1.0)
+        factor = small("factor", SLOTS, tag="late")
+        nc.scalar.activation(by_page(factor[:]), per_slot(sig[:]), ACT.Copy, scale=144.0)
+
+        val_codes = gather("val_codes", val_pool[:].bitcast(U32), U32, as_listed)
+        c0 = psum.tile([Q, SLOTS], F32, name="c0")
+        product(c0[:], rows_c, val_codes[:], val_bytes[VAL_PLANE:, :])
+
+        up = small("up")
+        up_sum = small("up_sum", 1)
+        nc.vector.scalar_tensor_tensor(up[:], sig[:], 1.0, sum_tb, ALU.mult, ALU.mult, accum_out=up_sum[:])
+        quota = sb.tile([P, PAGES + 1], F32, name="quota", tag="val_pool", align_bytes=64)
+        q0 = quota[:, :PAGES]
+        z = quota[:, PAGES:]
+        nc.vector.tensor_tensor(z, z_pos[:], log_sum[:], ALU.subtract)
+        nc.vector.tensor_tensor(q0, pos[:], log_sig[:], ALU.subtract)
+        inv_z = small("inv_z", 1)
+        nc.vector.reciprocal(inv_z[:], z)
+        shift = small("shift", 1)
+        nc.vector.tensor_scalar(shift[:], up_sum[:], inv_z[:], -1.0, ALU.mult, ALU.mult)
+        w = small("w")
+        nc.vector.scalar_tensor_tensor(w[:], q0, shift[:], up[:], ALU.mult, ALU.add)
+        slope = small("slope")
+        nc.vector.scalar_tensor_tensor(slope[:], sum_tb, shift[:], up[:], ALU.add, ALU.subtract)
+
+        drr = small("drr", SLOTS)
+        nc.vector.tensor_tensor(drr[:], c0[:], pa[:], ALU.mult)
+        dr = small("dr")
+        nc.vector.tensor_reduce(dr[:], by_page(drr[:]), AX.X, ALU.add)
+        r = small("r")
+        nc.vector.tensor_tensor(r[:], dr[:], inv_s[:], ALU.mult)
+        rq = small("rq")
+        mean_r = small("mean_r", 1)
+        nc.vector.scalar_tensor_tensor(rq[:], r[:], inv_z[:], q0, ALU.mult, ALU.mult, accum_out=mean_r[:])
+        rw = small("rw")
+        drift = small("drift", 1)
+        nc.vector.scalar_tensor_tensor(rw[:], r[:], inv_z[:], w[:], ALU.mult, ALU.mult, accum_out=drift[:])
+        local = small("local")
+        nc.vector.scalar_tensor_tensor(local[:], r[:], mean_r[:], slope[:], ALU.subtract, ALU.mult)
+        spread = small("spread", SLOTS)
+        nc.vector.tensor_scalar(by_page(spread[:]), per_slot(local[:]), drift[:], inv_z[:], ALU.subtract, ALU.mult)
+        nc.vector.tensor_tensor(placed[:].indirect(offsets[:]), spread[:], factor[:], ALU.mult)
+
+        first = 0
+        for width in OUT_WIDTHS:
+            cols = slice(first, first + width)
+            total = sb.tile([P, width], F32, name="total%d" % first)
+            nc.vector.tensor_tensor(total[:], base_sb[:, cols], placed[:, cols], ALU.add)
+            nc.sync.dma_start(out=out[:, cols], in_=total[:])
+            first = first + width

@@ -23,8 +23,7 @@ PAGE = 8
 RUNS = 4
 PAIR = PAGE // RUNS
 RUN = SLOTS // RUNS
-OUT_WIDTHS = (512, 512, 512, 512)
-VAL_PLANE = 4
+OUT_WIDTHS = (256, 512, 512, 512, 256)
 
 FLOPS = 4 * 2 * 512 * Q * SLOTS
 
@@ -39,7 +38,7 @@ def tile_attend_hvpagequotas_s_kernel(
         psum = ctx.enter_context(tc.psum_pool(name="psum", bufs=1))
 
         def small(name, cols=PAGES, tag=None):
-            return sb.tile([P, cols], F32, name=name, tag=tag or name)
+            return sb.tile([P, cols], F32, name=name, tag=tag or name, align_bytes=64)
 
         def per_slot(ap):
             return ap.unsqueeze(2).to_broadcast([P, PAGES, PAGE])
@@ -53,11 +52,11 @@ def tile_attend_hvpagequotas_s_kernel(
         offsets = lists.tile([P, SLOTS // 16], U16, name="offsets")
         nc.sync.dma_start(offsets[:], offs)
 
-        def load_scales(queue, name, scales, first_row):
+        def load_scales(queue, name, scales):
             plane = sb.tile([P, T], U8, name=name, align_bytes=64)
             nc.vector.memset(plane[:].bitcast(I32), 0)
             for quad in range(4):
-                r0 = 32 * quad + first_row
+                r0 = 32 * quad
                 queue.dma_start(
                     out=plane[r0 : r0 + 4, :].bitcast(I32), in_=scales[0, 4 * quad : 4 * quad + 4, :].bitcast(I32)
                 )
@@ -69,20 +68,20 @@ def tile_attend_hvpagequotas_s_kernel(
             return pool_words
 
         def load_rows(queue, name, rows):
-            raw = sb.tile([P, PACK, Q], F32, name=name, tag=name)
+            raw = sb.tile([P, PACK, Q], F32, name=name, tag=name, align_bytes=64)
             queue.dma_start(out=raw[:], in_=rows.rearrange("(p j) w -> p j w", j=PACK))
             return raw
 
-        key_pool = load_words("key_pool", keys_words)
-        key_plane = load_scales(nc.scalar, "key_plane", keys_scales, 0)
+        res = small("res", 1)
+        nc.sync.dma_start(out=res[:], in_=reserve)
         raw_a = load_rows(nc.sync, "raw_a", query)
+        key_plane = load_scales(nc.sync, "key_plane", keys_scales)
+        key_pool = load_words("key_pool", keys_words)
+        val_plane = load_scales(nc.sync, "val_plane", vals_scales)
         raw_b = load_rows(nc.sync, "raw_b", query2)
-        val_plane = load_scales(nc.sync, "val_plane", vals_scales, VAL_PLANE)
         raw_tb = load_rows(nc.sync, "raw_tb", dquery2)
         raw_c = load_rows(nc.sync, "raw_c", gout)
         val_pool = load_words("val_pool", vals_words)
-        res = small("res", 1)
-        nc.sync.dma_start(out=res[:], in_=reserve)
         base_sb = sb.tile([P, T], F32, name="base_sb")
         nc.sync.dma_start(out=base_sb[:], in_=base)
 
@@ -100,7 +99,7 @@ def tile_attend_hvpagequotas_s_kernel(
             return ap
 
         def quantize(name, raw):
-            grouped = sb.tile([P, Q, PACK], BF16, name=name + "_grouped", align_bytes=64)
+            grouped = sb.tile([P, Q, PACK], BF16, name=name + "_grouped", tag=name + "_grouped", align_bytes=64)
             nc.scalar.activation(grouped[:], raw[:].rearrange("p j w -> p w j"), ACT.Copy)
             codes = sb.tile([P, Q], U32, name=name + "_codes", align_bytes=64)
             scales = sb.tile([P, Q], U8, name=name + "_scales", align_bytes=64)
@@ -124,32 +123,32 @@ def tile_attend_hvpagequotas_s_kernel(
         key_codes = gather("key_codes", key_pool[:].bitcast(U32), U32, dealt)
         a = psum.tile([Q, SLOTS], F32, name="a")
         product(a[:], quantize("qa", raw_a), key_codes[:], key_bytes[:])
-        pairs = psum.tile([Q, 2, RUN], F32, name="pairs")
-        for side, (name, raw) in enumerate((("qb", raw_b), ("qt", raw_tb))):
+        pairs = []
+        for name, raw in (("qb", raw_b), ("qt", raw_tb)):
             rows = quantize(name, raw)
+            bank = psum.tile([Q, RUN], F32, name=name + "_pairs")
             for h in range(RUNS):
                 cols = slice(h * RUN, (h + 1) * RUN)
-                product(pairs[:, side, :], rows, key_codes[:, cols], key_bytes[:, cols], h == 0, h == RUNS - 1)
+                product(bank[:], rows, key_codes[:, cols], key_bytes[:, cols], h == 0, h == RUNS - 1)
+            pairs.append(bank[:].rearrange("p (g l) -> p g l", l=PAIR))
 
         val_bytes = gather("val_bytes", val_plane[:], U8, as_listed)
 
         rows_c = quantize("qc", raw_c)
-        top = small("top")
+        top = small("top", tag="qb_grouped")
         shifted = small("shifted", SLOTS, tag="exp_arg")
         nc.vector.tensor_reduce(top[:], dealt(a[:]), AX.XY, ALU.max)
+        sum_b = small("sum_b")[:]
+        nc.vector.tensor_reduce(sum_b, pairs[0], AX.X, ALU.add)
         nc.vector.tensor_tensor(
             shifted[:].rearrange("p (g h l) -> p g h l", h=RUNS, l=PAIR),
             dealt(a[:]),
             top[:].unsqueeze(2).unsqueeze(3).to_broadcast([P, PAGES, RUNS, PAIR]),
             ALU.subtract,
         )
-        pa = small("pa", SLOTS)
+        pa = small("pa", SLOTS, tag="raw_tb")
         nc.scalar.activation(pa[:], shifted[:], ACT.Exp)
 
-        sums = small("sums", 2 * PAGES)
-        nc.vector.tensor_reduce(sums[:], pairs[:].rearrange("p s (g l) -> p (s g) l", l=PAIR), AX.X, ALU.add)
-        sum_b = sums[:, :PAGES]
-        sum_tb = sums[:, PAGES:]
         th = small("th")
         nc.scalar.activation(th[:], sum_b, ACT.Tanh, scale=0.1875)
         pos = small("pos")
@@ -159,44 +158,42 @@ def tile_attend_hvpagequotas_s_kernel(
         nc.scalar.activation(abs_th[:], th[:], ACT.Abs)
         sig = small("sig")
         nc.scalar.activation(sig[:], th[:], ACT.Identity, bias=half[:], scale=0.5)
-        z_pos = small("z_pos", 1)
-        nc.scalar.activation(z_pos[:], pos_sum[:], ACT.Identity, bias=res[:], scale=1.0)
         log_sig = small("log_sig", tag="exp_arg")
         log_sum = small("log_sum", 1)
         nc.scalar.activation(log_sig[:], abs_th[:], ACT.Ln, bias=half[:], scale=0.5, accum_out=log_sum[:])
 
-        s = small("s")
-        nc.vector.tensor_reduce(s[:], by_page(pa[:]), AX.X, ALU.add)
-        inv_s = small("inv_s")
-        log_s = small("log_s", tag="late")
-        nc.scalar.activation(log_s[:], s[:], ACT.Ln)
-        nc.scalar.activation(inv_s[:], log_s[:], ACT.Exp, scale=-1.0)
-        factor = small("factor", SLOTS, tag="late")
+        val_codes = gather("val_codes", val_pool[:].bitcast(U32), U32, as_listed)
+        late = sb.tile([P, 2 * PAGES + 1], F32, name="late_v", tag="val_pool", align_bytes=64)
+        s = late[:, :PAGES]
+        nc.vector.tensor_reduce(s, by_page(pa[:]), AX.X, ALU.add)
+        factor = small("factor", SLOTS, tag="raw_c")
         nc.scalar.activation(by_page(factor[:]), per_slot(sig[:]), ACT.Copy, scale=144.0)
 
-        val_codes = gather("val_codes", val_pool[:].bitcast(U32), U32, as_listed)
         c0 = psum.tile([Q, SLOTS], F32, name="c0")
-        product(c0[:], rows_c, val_codes[:], val_bytes[VAL_PLANE:, :])
+        product(c0[:], rows_c, val_codes[:], val_bytes[:])
 
+        sum_tb = small("sum_tb")[:]
+        nc.vector.tensor_reduce(sum_tb, pairs[1], AX.X, ALU.add)
         up = small("up")
         up_sum = small("up_sum", 1)
         nc.vector.scalar_tensor_tensor(up[:], sig[:], 1.0, sum_tb, ALU.mult, ALU.mult, accum_out=up_sum[:])
-        quota = sb.tile([P, PAGES + 1], F32, name="quota", tag="val_pool", align_bytes=64)
-        q0 = quota[:, :PAGES]
-        z = quota[:, PAGES:]
-        nc.vector.tensor_tensor(z, z_pos[:], log_sum[:], ALU.subtract)
+        q0 = late[:, PAGES : 2 * PAGES]
+        z = late[:, 2 * PAGES :]
+        nc.vector.tensor_scalar(z, pos_sum[:], res[:], log_sum[:], ALU.add, ALU.subtract)
         nc.vector.tensor_tensor(q0, pos[:], log_sig[:], ALU.subtract)
         inv_z = small("inv_z", 1)
         nc.vector.reciprocal(inv_z[:], z)
         shift = small("shift", 1)
         nc.vector.tensor_scalar(shift[:], up_sum[:], inv_z[:], -1.0, ALU.mult, ALU.mult)
+        drr = small("drr", SLOTS)
+        nc.vector.tensor_tensor(drr[:], c0[:], pa[:], ALU.mult)
+        inv_s = small("inv_s")
+        nc.vector.reciprocal(inv_s[:], s)
         w = small("w")
         nc.vector.scalar_tensor_tensor(w[:], q0, shift[:], up[:], ALU.mult, ALU.add)
         slope = small("slope")
         nc.vector.scalar_tensor_tensor(slope[:], sum_tb, shift[:], up[:], ALU.add, ALU.subtract)
 
-        drr = small("drr", SLOTS)
-        nc.vector.tensor_tensor(drr[:], c0[:], pa[:], ALU.mult)
         dr = small("dr")
         nc.vector.tensor_reduce(dr[:], by_page(drr[:]), AX.X, ALU.add)
         r = small("r")

@@ -24,6 +24,7 @@ RUNS = 4
 PAIR = PAGE // RUNS
 RUN = SLOTS // RUNS
 OUT_WIDTHS = (256, 512, 512, 512, 256)
+VAL_PLANE = 4
 
 FLOPS = 4 * 2 * 512 * Q * SLOTS
 
@@ -52,14 +53,12 @@ def tile_attend_hvpagequotas_s_kernel(
         offsets = lists.tile([P, SLOTS // 16], U16, name="offsets")
         nc.sync.dma_start(offsets[:], offs)
 
-        def load_scales(queue, name, scales):
+        def load_scales(queue, name, scales, first_row):
             plane = sb.tile([P, T], U8, name=name, align_bytes=64)
             nc.vector.memset(plane[:].bitcast(I32), 0)
-            for quad in range(4):
-                r0 = 32 * quad
-                queue.dma_start(
-                    out=plane[r0 : r0 + 4, :].bitcast(I32), in_=scales[0, 4 * quad : 4 * quad + 4, :].bitcast(I32)
-                )
+            for r in range(4):
+                rows = plane[first_row + r : P : 32, :]
+                queue.dma_start(out=rows.bitcast(I32), in_=scales[0, r:16:4, :].bitcast(I32))
             return plane
 
         def load_words(name, words):
@@ -75,9 +74,9 @@ def tile_attend_hvpagequotas_s_kernel(
         res = small("res", 1)
         nc.sync.dma_start(out=res[:], in_=reserve)
         raw_a = load_rows(nc.sync, "raw_a", query)
-        key_plane = load_scales(nc.sync, "key_plane", keys_scales)
+        key_plane = load_scales(nc.sync, "key_plane", keys_scales, 0)
         key_pool = load_words("key_pool", keys_words)
-        val_plane = load_scales(nc.sync, "val_plane", vals_scales)
+        val_plane = load_scales(nc.sync, "val_plane", vals_scales, VAL_PLANE)
         raw_b = load_rows(nc.sync, "raw_b", query2)
         raw_tb = load_rows(nc.sync, "raw_tb", dquery2)
         raw_c = load_rows(nc.sync, "raw_c", gout)
@@ -158,10 +157,14 @@ def tile_attend_hvpagequotas_s_kernel(
         nc.scalar.activation(abs_th[:], th[:], ACT.Abs)
         sig = small("sig")
         nc.scalar.activation(sig[:], th[:], ACT.Identity, bias=half[:], scale=0.5)
+        z_pos = small("z_pos", 1)
+        nc.scalar.activation(z_pos[:], pos_sum[:], ACT.Identity, bias=res[:], scale=1.0)
         log_sig = small("log_sig", tag="exp_arg")
         log_sum = small("log_sum", 1)
         nc.scalar.activation(log_sig[:], abs_th[:], ACT.Ln, bias=half[:], scale=0.5, accum_out=log_sum[:])
 
+        z = small("z", 1)
+        nc.scalar.activation(z[:], log_sum[:], ACT.Identity, bias=z_pos[:], scale=-1.0)
         val_codes = gather("val_codes", val_pool[:].bitcast(U32), U32, as_listed)
         late = sb.tile([P, 2 * PAGES + 1], F32, name="late_v", tag="val_pool", align_bytes=64)
         s = late[:, :PAGES]
@@ -170,29 +173,27 @@ def tile_attend_hvpagequotas_s_kernel(
         nc.scalar.activation(by_page(factor[:]), per_slot(sig[:]), ACT.Copy, scale=144.0)
 
         c0 = psum.tile([Q, SLOTS], F32, name="c0")
-        product(c0[:], rows_c, val_codes[:], val_bytes[:])
+        product(c0[:], rows_c, val_codes[:], val_bytes[VAL_PLANE:, :])
 
         sum_tb = small("sum_tb")[:]
         nc.vector.tensor_reduce(sum_tb, pairs[1], AX.X, ALU.add)
         up = small("up")
         up_sum = small("up_sum", 1)
-        nc.vector.scalar_tensor_tensor(up[:], sig[:], 1.0, sum_tb, ALU.mult, ALU.mult, accum_out=up_sum[:])
+        nc.vector.scalar_tensor_tensor(up[:], sig[:], -1.0, sum_tb, ALU.mult, ALU.mult, accum_out=up_sum[:])
         q0 = late[:, PAGES : 2 * PAGES]
-        z = late[:, 2 * PAGES :]
-        nc.vector.tensor_scalar(z, pos_sum[:], res[:], log_sum[:], ALU.add, ALU.subtract)
         nc.vector.tensor_tensor(q0, pos[:], log_sig[:], ALU.subtract)
-        inv_z = small("inv_z", 1)
-        nc.vector.reciprocal(inv_z[:], z)
+        inv_z = late[:, 2 * PAGES :]
+        nc.vector.reciprocal(inv_z, z[:])
         shift = small("shift", 1)
-        nc.vector.tensor_scalar(shift[:], up_sum[:], inv_z[:], -1.0, ALU.mult, ALU.mult)
+        nc.scalar.activation(shift[:], up_sum[:], ACT.Copy, scale=inv_z)
         drr = small("drr", SLOTS)
         nc.vector.tensor_tensor(drr[:], c0[:], pa[:], ALU.mult)
         inv_s = small("inv_s")
         nc.vector.reciprocal(inv_s[:], s)
         w = small("w")
-        nc.vector.scalar_tensor_tensor(w[:], q0, shift[:], up[:], ALU.mult, ALU.add)
+        nc.vector.scalar_tensor_tensor(w[:], q0, shift[:], up[:], ALU.mult, ALU.subtract)
         slope = small("slope")
-        nc.vector.scalar_tensor_tensor(slope[:], sum_tb, shift[:], up[:], ALU.add, ALU.subtract)
+        nc.vector.scalar_tensor_tensor(slope[:], sum_tb, shift[:], up[:], ALU.add, ALU.add)
 
         dr = small("dr")
         nc.vector.tensor_reduce(dr[:], by_page(drr[:]), AX.X, ALU.add)
@@ -200,14 +201,14 @@ def tile_attend_hvpagequotas_s_kernel(
         nc.vector.tensor_tensor(r[:], dr[:], inv_s[:], ALU.mult)
         rq = small("rq")
         mean_r = small("mean_r", 1)
-        nc.vector.scalar_tensor_tensor(rq[:], r[:], inv_z[:], q0, ALU.mult, ALU.mult, accum_out=mean_r[:])
+        nc.vector.scalar_tensor_tensor(rq[:], r[:], inv_z, q0, ALU.mult, ALU.mult, accum_out=mean_r[:])
         rw = small("rw")
         drift = small("drift", 1)
-        nc.vector.scalar_tensor_tensor(rw[:], r[:], inv_z[:], w[:], ALU.mult, ALU.mult, accum_out=drift[:])
+        nc.vector.scalar_tensor_tensor(rw[:], r[:], inv_z, w[:], ALU.mult, ALU.mult, accum_out=drift[:])
         local = small("local")
         nc.vector.scalar_tensor_tensor(local[:], r[:], mean_r[:], slope[:], ALU.subtract, ALU.mult)
         spread = small("spread", SLOTS)
-        nc.vector.tensor_scalar(by_page(spread[:]), per_slot(local[:]), drift[:], inv_z[:], ALU.subtract, ALU.mult)
+        nc.vector.tensor_scalar(by_page(spread[:]), per_slot(local[:]), drift[:], inv_z, ALU.subtract, ALU.mult)
         nc.vector.tensor_tensor(placed[:].indirect(offsets[:]), spread[:], factor[:], ALU.mult)
 
         first = 0

from contextlib import ExitStack

import concourse.mybir as mybir

F32 = mybir.dt.float32
BF16 = mybir.dt.bfloat16
I32 = mybir.dt.int32
U32 = mybir.dt.uint32
U16 = mybir.dt.uint16
U8 = mybir.dt.uint8
FP8X4 = mybir.dt.float8_e4m3fn_x4
ALU = mybir.AluOpType
ACT = mybir.ActivationFunctionType
AX = mybir.AxisListType

P = 128
PACK = 4
T = 2048
SLOTS = 512
Q = 128
PAGES = 64
PAGE = 8
RUNS = 4
PAIR = PAGE // RUNS
RUN = SLOTS // RUNS
OUT_WIDTHS = (256, 512, 512, 512, 256)
VAL_PLANE = 4

FLOPS = 4 * 2 * 512 * Q * SLOTS


def tile_attend_hvpagequotas_s_kernel(
    tc, query, query2, keys_words, keys_scales, reserve, gout, vals_words, vals_scales, dquery2, base, offs, out
):
    nc = tc.nc
    with ExitStack() as ctx:
        lists = ctx.enter_context(tc.tile_pool(name="lists", bufs=1))
        sb = ctx.enter_context(tc.tile_pool(name="sb", bufs=1))
        psum = ctx.enter_context(tc.psum_pool(name="psum", bufs=1))

        def small(name, cols=PAGES, tag=None):
            return sb.tile([P, cols], F32, name=name, tag=tag or name, align_bytes=64)

        def per_slot(ap):
            return ap.unsqueeze(2).to_broadcast([P, PAGES, PAGE])

        def by_page(ap):
            return ap.rearrange("p (g j) -> p g j", j=PAGE)

        def dealt(ap):
            return ap.rearrange("p (h g l) -> p g h l", h=RUNS, l=PAIR)

        offsets = lists.tile([P, SLOTS // 16], U16, name="offsets")
        nc.sync.dma_start(offsets[:], offs)

        def load_scales(queue, name, scales, first_row):
            plane = sb.tile([P, T], U8, name=name, align_bytes=64)
            nc.vector.memset(plane[:].bitcast(I32), 0)
            for r in range(4):
                rows = plane[first_row + r : P : 32, :]
                queue.dma_start(out=rows.bitcast(I32), in_=scales[0, r:16:4, :].bitcast(I32))
            return plane

        def load_words(name, words):
            pool_words = sb.tile([P, T], I32, name=name, tag=name, align_bytes=64)
            nc.sync.dma_start(out=pool_words[:], in_=words[0].rearrange("p n t -> p (n t)").bitcast(I32))
            return pool_words

        def load_rows(queue, name, rows):
            raw = sb.tile([P, PACK, Q], F32, name=name, tag=name, align_bytes=64)
            queue.dma_start(out=raw[:], in_=rows.rearrange("(p j) w -> p j w", j=PACK))
            return raw

        res = small("res", 1)
        nc.sync.dma_start(out=res[:], in_=reserve)
        raw_a = load_rows(nc.sync, "raw_a", query)
        key_plane = load_scales(nc.sync, "key_plane", keys_scales, 0)
        key_pool = load_words("key_pool", keys_words)
        val_plane = load_scales(nc.sync, "val_plane", vals_scales, VAL_PLANE)
        raw_b = load_rows(nc.sync, "raw_b", query2)
        raw_tb = load_rows(nc.sync, "raw_tb", dquery2)
        raw_c = load_rows(nc.sync, "raw_c", gout)
        val_pool = load_words("val_pool", vals_words)
        base_sb = sb.tile([P, T], F32, name="base_sb")
        nc.sync.dma_start(out=base_sb[:], in_=base)

        placed = sb.tile([P, T], F32, name="placed")
        nc.vector.memset(placed[:], 0.0)
        half = small("half", 1)
        nc.vector.memset(half[:], 0.5)

        def gather(name, window, dtype, order):
            picked = sb.tile([P, SLOTS], dtype, name=name, align_bytes=64)
            nc.vector.tensor_copy(order(picked[:]), window.indirect(offsets[:]))
            return picked

        def as_listed(ap):
            return ap

        def quantize(name, raw):
            grouped = sb.tile([P, Q, PACK], BF16, name=name + "_grouped", tag=name + "_grouped", align_bytes=64)
            nc.scalar.activation(grouped[:], raw[:].rearrange("p j w -> p w j"), ACT.Copy)
            codes = sb.tile([P, Q], U32, name=name + "_codes", align_bytes=64)
            scales = sb.tile([P, Q], U8, name=name + "_scales", align_bytes=64)
            nc.vector.quantize_mx(
                out=codes[:].bitcast(FP8X4), scales=scales[:], in_=grouped[:].rearrange("p w j -> p (w j)")
            )
            return codes, scales

        def product(acc, rows, words, plane, start=True, stop=True):
            nc.tensor.matmul_mx(
                out=acc,
                lhsT=rows[0][:].bitcast(FP8X4),
                lhsT_scale=rows[1][:],
                rhs=words.bitcast(FP8X4),
                rhs_scale=plane,
                start=start,
                stop=stop,
            )

        key_bytes = gather("key_bytes", key_plane[:], U8, dealt)
        key_codes = gather("key_codes", key_pool[:].bitcast(U32), U32, dealt)
        a = psum.tile([Q, SLOTS], F32, name="a")
        product(a[:], quantize("qa", raw_a), key_codes[:], key_bytes[:])
        pairs = []
        for name, raw in (("qb", raw_b), ("qt", raw_tb)):
            rows = quantize(name, raw)
            bank = psum.tile([Q, RUN], F32, name=name + "_pairs")
            for h in range(RUNS):
                cols = slice(h * RUN, (h + 1) * RUN)
                product(bank[:], rows, key_codes[:, cols], key_bytes[:, cols], h == 0, h == RUNS - 1)
            pairs.append(bank[:].rearrange("p (g l) -> p g l", l=PAIR))

        val_bytes = gather("val_bytes", val_plane[:], U8, as_listed)

        rows_c = quantize("qc", raw_c)
        top = small("top", tag="qb_grouped")
        shifted = small("shifted", SLOTS, tag="exp_arg")
        nc.vector.tensor_reduce(top[:], dealt(a[:]), AX.XY, ALU.max)
        sum_b = small("sum_b")[:]
        nc.vector.tensor_reduce(sum_b, pairs[0], AX.X, ALU.add)
        nc.vector.tensor_tensor(
            shifted[:].rearrange("p (g h l) -> p g h l", h=RUNS, l=PAIR),
            dealt(a[:]),
            top[:].unsqueeze(2).unsqueeze(3).to_broadcast([P, PAGES, RUNS, PAIR]),
            ALU.subtract,
        )
        pa = small("pa", SLOTS, tag="raw_tb")
        nc.scalar.activation(pa[:], shifted[:], ACT.Exp)

        th = small("th")
        nc.scalar.activation(th[:], sum_b, ACT.Tanh, scale=0.1875)
        pos = small("pos")
        pos_sum = small("pos_sum", 1)
        nc.scalar.activation(pos[:], sum_b, ACT.Relu, scale=0.375, accum_out=pos_sum[:])
        abs_th = small("abs_th", tag="raw_c")
        nc.scalar.activation(abs_th[:], th[:], ACT.Abs)
        sig = small("sig")
        nc.scalar.activation(sig[:], th[:], ACT.Identity, bias=half[:], scale=0.5)
        z_pos = small("z_pos", 1)
        nc.scalar.activation(z_pos[:], pos_sum[:], ACT.Identity, bias=res[:], scale=1.0)
        log_sig = small("log_sig", tag="exp_arg")
        log_sum = small("log_sum", 1)
        nc.scalar.activation(log_sig[:], abs_th[:], ACT.Ln, bias=half[:], scale=0.5, accum_out=log_sum[:])

        z = small("z", 1)
        nc.scalar.activation(z[:], log_sum[:], ACT.Identity, bias=z_pos[:], scale=-1.0)
        val_codes = gather("val_codes", val_pool[:].bitcast(U32), U32, as_listed)
        late = sb.tile([P, 2 * PAGES + 1], F32, name="late_v", tag="val_pool", align_bytes=64)
        s = late[:, :PAGES]
        nc.vector.tensor_reduce(s, by_page(pa[:]), AX.X, ALU.add)
        factor = small("factor", SLOTS, tag="raw_c")
        nc.scalar.activation(by_page(factor[:]), per_slot(sig[:]), ACT.Copy, scale=144.0)

        c0 = psum.tile([Q, SLOTS], F32, name="c0")
        product(c0[:], rows_c, val_codes[:], val_bytes[VAL_PLANE:, :])

        sum_tb = small("sum_tb")[:]
        nc.vector.tensor_reduce(sum_tb, pairs[1], AX.X, ALU.add)
        up = small("up")
        up_sum = small("up_sum", 1)
        nc.vector.scalar_tensor_tensor(up[:], sig[:], -1.0, sum_tb, ALU.mult, ALU.mult, accum_out=up_sum[:])
        q0 = late[:, PAGES : 2 * PAGES]
        nc.vector.tensor_tensor(q0, pos[:], log_sig[:], ALU.subtract)
        inv_z = late[:, 2 * PAGES :]
        nc.vector.reciprocal(inv_z, z[:])
        shift = small("shift", 1)
        nc.scalar.activation(shift[:], up_sum[:], ACT.Copy, scale=inv_z)
        drr = small("drr", SLOTS)
        nc.vector.tensor_tensor(drr[:], c0[:], pa[:], ALU.mult)
        inv_s = small("inv_s")
        nc.vector.reciprocal(inv_s[:], s)
        w = small("w")
        nc.vector.scalar_tensor_tensor(w[:], q0, shift[:], up[:], ALU.mult, ALU.subtract)
        slope = small("slope")
        nc.vector.scalar_tensor_tensor(slope[:], sum_tb, shift[:], up[:], ALU.add, ALU.add)

        dr = small("dr")
        nc.vector.tensor_reduce(dr[:], by_page(drr[:]), AX.X, ALU.add)
        r = small("r")
        nc.vector.tensor_tensor(r[:], dr[:], inv_s[:], ALU.mult)
        rq = small("rq")
        mean_r = small("mean_r", 1)
        nc.vector.scalar_tensor_tensor(rq[:], r[:], inv_z, q0, ALU.mult, ALU.mult, accum_out=mean_r[:])
        rw = small("rw")
        drift = small("drift", 1)
        nc.vector.scalar_tensor_tensor(rw[:], r[:], inv_z, w[:], ALU.mult, ALU.mult, accum_out=drift[:])
        local = small("local")
        nc.vector.scalar_tensor_tensor(local[:], r[:], mean_r[:], slope[:], ALU.subtract, ALU.mult)
        spread = small("spread", SLOTS)
        nc.vector.tensor_scalar(by_page(spread[:]), per_slot(local[:]), drift[:], inv_z, ALU.subtract, ALU.mult)
        nc.vector.tensor_tensor(placed[:].indirect(offsets[:]), spread[:], factor[:], ALU.mult)

        first = 0
        for width in OUT_WIDTHS:
            cols = slice(first, first + width)
            total = sb.tile([P, width], F32, name="total%d" % first)
            nc.vector.tensor_tensor(total[:], base_sb[:, cols], placed[:, cols], ALU.add)
            nc.sync.dma_start(out=out[:, cols], in_=total[:])
            first = first + width
